import numpy as np
import ml_dtypes


def mxq(x, axis, fmt="e4m3"):
    dtype, down = {"e4m3": (ml_dtypes.float8_e4m3fn, 7), "e5m2": (ml_dtypes.float8_e5m2, 14)}[fmt]
    v = np.moveaxis(np.asarray(x, np.float32).astype(ml_dtypes.bfloat16).astype(np.float64), axis, -1)
    blocks = v.reshape(v.shape[:-1] + (-1, 32))
    amax = np.abs(blocks).max(-1, keepdims=True)
    byte = np.maximum(np.where(amax > 0, np.frexp(amax)[1] - 1 + 127, 0) - down, 1)
    scale = np.exp2(byte - 127.0)
    codes = (blocks / scale).astype(np.float32).astype(dtype).astype(np.float64)
    return np.moveaxis((codes * scale).reshape(v.shape), -1, axis)


WIDE = False


def mx_kscale(k):
    if not WIDE:
        return np.ones(k)
    levels = np.array([10, -10, 5, -5, 0])
    if k % 512:
        return np.exp2(np.random.permutation(np.resize(levels, k // 32))).repeat(32)
    a = np.empty((k // 512, 16))
    for p in range(k // 512):
        a[p, :8] = np.random.permutation(np.resize(levels, 8))
        for g in range(8):
            far = levels[np.abs(levels - a[p, g]) >= 10]
            a[p, g + 8] = far[np.random.randint(len(far))]
    return np.exp2(a.ravel()).repeat(32)


def f64(x):
    return np.asarray(x).astype(np.float64)


E2M1 = np.array([0.0, 0.5, 1.0, 1.5, 2.0, 3.0, 4.0, 6.0, -0.0, -0.5, -1.0, -1.5, -2.0, -3.0, -4.0, -6.0])


def pack_weight(w, fmt):
    k, n = w.shape
    w = f64(np.asarray(w, np.float32).astype(ml_dtypes.bfloat16)).reshape(k // 32, 32, n)
    amax = np.abs(w).max(1)
    if fmt == "e4m3":
        byte = np.frexp(amax)[1] - 1 + 127 - 7
    else:
        mant, ex = np.frexp(amax / 6.0)
        byte = np.where(mant > 0.5, ex, ex - 1) + 127
    byte = np.clip(np.where(amax > 0, byte, 1), 1, 254)
    scaled = (w * np.exp2(127.0 - byte)[:, None, :]).reshape(k, n).astype(np.float32)
    by_word = np.ascontiguousarray(scaled.reshape(k // 512, 128, 4, n).transpose(0, 1, 3, 2))
    if fmt == "e4m3":
        words = by_word.astype(ml_dtypes.float8_e4m3fn).view(np.uint8)
    else:
        c = by_word.astype(ml_dtypes.float4_e2m1fn).view(np.uint8) & 0xF
        words = (c[..., 0::2] | (c[..., 1::2] << 4)).reshape(k // 512, 128, 2 * n)
    return np.ascontiguousarray(words), np.ascontiguousarray(byte.astype(np.uint8).reshape(k // 512, 16, n))


def unpack_weight(words, scales, fmt):
    g, _, n = scales.shape
    words = np.ascontiguousarray(words).reshape(g, 128, n, -1)
    if fmt == "e4m3":
        vals = words.view(ml_dtypes.float8_e4m3fn).astype(np.float64)
    else:
        nib = np.empty((g, 128, n, 4), np.uint8)
        nib[..., 0::2] = words & 0xF
        nib[..., 1::2] = words >> 4
        vals = E2M1[nib]
    vals = vals * np.repeat(np.exp2(scales.astype(np.float64) - 127.0), 8, axis=1)[..., None]
    return vals.transpose(0, 1, 3, 2).reshape(g * 512, n)


def bf(x):
    return np.asarray(x, np.float32).astype(ml_dtypes.bfloat16)


def planes(Y):
    r, m = Y.shape
    b = f64(bf(Y)).reshape(r // 32, 32, m)
    amax = np.abs(b).max(1)
    byte = np.clip(np.where(amax > 0, np.frexp(amax)[1] - 1 + 127 - 7, 1), 1, 254)
    codes = (b * np.exp2(127.0 - byte)[:, None, :]).reshape(r, m).astype(np.float32).astype(ml_dtypes.float8_e4m3fn).view(np.uint8)
    words = codes.reshape(r // 512, 128, 4, m).transpose(0, 1, 3, 2)
    return np.ascontiguousarray(words), np.ascontiguousarray(byte.astype(np.uint8).reshape(r // 512, 16, m))


K, L, T, R, N = 1024, 512, 512, 512, 512


def setup_inputs():
    n = np.random.standard_normal
    fk = mx_kscale(K)
    fr = mx_kscale(R)
    fl = mx_kscale(L)
    xtp = pack_weight(n((K, T)) / fk[:, None], "e2m1")
    wap = pack_weight(n((K, R)) * 1 / np.sqrt(K) * fk[:, None] * fr, "e4m3")
    cqp = pack_weight(n((L, T)) / fl[:, None], "e2m1")
    wcp = pack_weight(n((L, R)) * 1 / np.sqrt(L) * fl[:, None] * fr, "e4m3")
    wbp = pack_weight(n((R, N)) * 1 / np.sqrt(R) / fr[:, None], "e2m1")
    wyp = pack_weight(n((K, N)) * 1 / np.sqrt(K) * fk[:, None], "e4m3")
    return {
        "xt_words": xtp[0],
        "xt_scales": xtp[1],
        "wa_words": wap[0],
        "wa_scales": wap[1],
        "cq_words": cqp[0],
        "cq_scales": cqp[1],
        "wc_words": wcp[0],
        "wc_scales": wcp[1],
        "wb_words": wbp[0],
        "wb_scales": wbp[1],
        "wy_words": wyp[0],
        "wy_scales": wyp[1],
    }


def reference(xt_words, xt_scales, wa_words, wa_scales, cq_words, cq_scales, wc_words, wc_scales, wb_words, wb_scales, wy_words, wy_scales):
    xtu = unpack_weight(xt_words, xt_scales, "e2m1")
    wau = unpack_weight(wa_words, wa_scales, "e4m3")
    cqu = unpack_weight(cq_words, cq_scales, "e2m1")
    wcu = unpack_weight(wc_words, wc_scales, "e4m3")
    wbu = unpack_weight(wb_words, wb_scales, "e2m1")
    wyu = unpack_weight(wy_words, wy_scales, "e4m3")
    z = wau.T @ xtu + wcu.T @ cqu
    hid = np.maximum(z, 0.0)
    hidq = mxq(hid, 0, "e4m3")
    y = wbu.T @ hidq + wyu.T @ xtu
    words, scales = planes(y)
    return y, words, scales

@@ -1,0 +1,193 @@
+from contextlib import ExitStack
+
+import concourse.mybir as mybir
+
+K, L, T, R, N = 1024, 512, 512, 512, 512
+FLOPS = 2 * T * (R * (K + L) + N * (R + K))
+
+F32 = mybir.dt.float32
+BF16 = mybir.dt.bfloat16
+I32 = mybir.dt.int32
+U32 = mybir.dt.uint32
+U8 = mybir.dt.uint8
+E4M3 = mybir.dt.float8_e4m3fn_x4
+E2M1 = mybir.dt.float4_e2m1fn_x4
+ACT = mybir.ActivationFunctionType
+
+P = 128
+PACK = 4
+W = 512
+TC = 128
+CHUNKS = T // TC
+
+
+def tile_mix_conditioned_hidden_pl_kernel(
+    tc, xt_words, xt_scales, wa_words, wa_scales, cq_words, cq_scales, wc_words, wc_scales,
+    wb_words, wb_scales, wy_words, wy_scales, out_0, out_1, out_2,
+):
+    nc = tc.nc
+    with ExitStack() as ctx:
+        sb = ctx.enter_context(tc.tile_pool(name="sb", bufs=1))
+        psum = ctx.enter_context(tc.psum_pool(name="psum", bufs=1))
+        ctx.enter_context(tc.manual_schedule())
+
+        def tile(name, shape, dtype):
+            return sb.tile(shape, dtype, name=name, align_bytes=64)
+
+        def scale_tile(name, passes):
+            plane = tile(name, [P, passes, W], U8)
+            nc.vector.memset(plane[:].rearrange("p z c -> p (z c)").bitcast(I32), 0)
+            return plane
+
+        def load_scales(queue, plane, scales, q):
+            queue.dma_start(
+                out=plane[32 * q : 32 * q + 4, :, :].bitcast(I32),
+                in_=scales[:, 4 * q : 4 * q + 4, :].rearrange("z r c -> r z c").bitcast(I32),
+            )
+
+        def load_e4m3(name, words, z):
+            raw = tile(name, [P, W], U32)
+            nc.sync.dma_start(out=raw[:].bitcast(I32), in_=words[z].rearrange("p c r -> p (c r)").bitcast(I32))
+            return raw
+
+        def load_e2m1(name, words, z):
+            raw = tile(name, [P, 2 * W], U8)
+            nc.sync.dma_start(out=raw[:].bitcast(I32), in_=words[z].bitcast(I32))
+            return raw
+
+        def deal_e4m3(name, raw):
+            dealt = tile(name, [P, W], U32)
+            nc.vector.tensor_copy(
+                out=dealt[:].bitcast(I32).rearrange("p (j b i) -> p b j i", j=PACK, i=4),
+                in_=raw[:].bitcast(I32).rearrange("p (b i j) -> p b j i", j=PACK, i=4),
+            )
+            return dealt
+
+        def deal_e2m1(name, raw):
+            dealt = tile(name, [P, 2 * W], U8)
+            nc.vector.tensor_copy(
+                out=dealt[:].rearrange("p (j m e) -> p j m e", j=PACK, e=2),
+                in_=raw[:].rearrange("p (m j e) -> p j m e", j=PACK, e=2),
+            )
+            return dealt
+
+        def deal_scales(name, plane, z):
+            dealt = tile(name, [P, W], U8)
+            nc.vector.tensor_copy(
+                out=dealt[:].rearrange("p (j m) -> p j m", j=PACK),
+                in_=plane[:, z, :].rearrange("p (m j) -> p j m", j=PACK),
+            )
+            return dealt
+
+        def cols(i):
+            return slice(i * P, (i + 1) * P)
+
+        def cols2(i):
+            return slice(2 * i * P, 2 * (i + 1) * P)
+
+        wa_sraw = scale_tile("wa_sraw", 2)
+        xt_s = scale_tile("xt_s", 2)
+        cq_s = scale_tile("cq_s", 1)
+        wc_sraw = scale_tile("wc_sraw", 1)
+        wy_sraw = scale_tile("wy_sraw", 2)
+        wb_sraw = scale_tile("wb_sraw", 1)
+
+        wa_raw = [load_e4m3("wa_raw0", wa_words, 0)]
+        xt = [load_e2m1("xt0", xt_words, 0)]
+        for q in range(4):
+            load_scales(nc.scalar, wa_sraw, wa_scales, q)
+        for q in range(2):
+            load_scales(nc.sync, xt_s, xt_scales, q)
+        for q in range(2, 4):
+            load_scales(nc.gpsimd, xt_s, xt_scales, q)
+        for q in range(2):
+            load_scales(nc.gpsimd, cq_s, cq_scales, q)
+        wa_raw.append(load_e4m3("wa_raw1", wa_words, 1))
+        xt.append(load_e2m1("xt1", xt_words, 1))
+        for q in range(4):
+            load_scales(nc.scalar, wc_sraw, wc_scales, q)
+        wc_raw = load_e4m3("wc_raw", wc_words, 0)
+        cq = load_e2m1("cq", cq_words, 0)
+        for q in range(2, 4):
+            load_scales(nc.sync, cq_s, cq_scales, q)
+        for q in range(4):
+            load_scales(nc.sync, wy_sraw, wy_scales, q)
+        wy_raw = [load_e4m3("wy_raw%d" % z, wy_words, z) for z in range(2)]
+        wb_raw = load_e2m1("wb_raw", wb_words, 0)
+        for q in range(4):
+            load_scales(nc.sync, wb_sraw, wb_scales, q)
+
+        wa_s = [deal_scales("wa_s0", wa_sraw, 0)]
+        wa = [deal_e4m3("wa0", wa_raw[0])]
+        wa_s.append(deal_scales("wa_s1", wa_sraw, 1))
+        wa.append(deal_e4m3("wa1", wa_raw[1]))
+        wc_s = deal_scales("wc_s", wc_sraw, 0)
+        wc = deal_e4m3("wc", wc_raw)
+        wy_s = [deal_scales("wy_s%d" % z, wy_sraw, z) for z in range(2)]
+        wy = [deal_e4m3("wy%d" % z, wy_raw[z]) for z in range(2)]
+        wb = deal_e2m1("wb", wb_raw)
+        wb_s = deal_scales("wb_s", wb_sraw, 0)
+
+        z_bank = [psum.tile([P, PACK, TC], F32, name="z%d" % c) for c in range(CHUNKS)]
+        y_bank = [psum.tile([P, PACK, TC], F32, name="y%d" % c) for c in range(CHUNKS)]
+
+        def fp8_by_fp4(bank, w, w_s, x, x_s, z, c, first, last):
+            for j in range(PACK):
+                nc.tensor.matmul_mx(
+                    out=bank[:, j, :],
+                    lhsT=w[:, cols(j)].bitcast(E4M3),
+                    lhsT_scale=w_s[:, cols(j)],
+                    rhs=x[:, cols2(c)].bitcast(E2M1),
+                    rhs_scale=x_s[:, z, cols(c)],
+                    start=first and j == 0,
+                    stop=last and j == PACK - 1,
+                )
+
+        for z in range(2):
+            for c in range(CHUNKS):
+                fp8_by_fp4(z_bank[c], wa[z], wa_s[z], xt[z], xt_s, z, c, z == 0, False)
+        hid_q = []
+        hid_s = []
+        for c in range(CHUNKS):
+            fp8_by_fp4(z_bank[c], wc, wc_s, cq, cq_s, 0, c, False, True)
+            hid = tile("hid%d" % c, [P, TC, PACK], BF16)
+            nc.scalar.activation(out=hid[:], in_=z_bank[c][:].rearrange("p j t -> p t j"), func=ACT.Relu)
+            codes = tile("hid_q%d" % c, [P, TC], U32)
+            plane = tile("hid_s%d" % c, [P, TC], U8)
+            nc.vector.quantize_mx(out=codes[:].bitcast(E4M3), scales=plane[:], in_=hid[:].rearrange("p t j -> p (t j)"))
+            hid_q.append(codes)
+            hid_s.append(plane)
+
+        out_rows = out_0.rearrange("(p j) t -> p j t", j=PACK)
+        out_words = out_1[0].rearrange("p c r -> p (c r)").bitcast(I32)
+        y_s = tile("y_s", [P, T], U8)
+        for c in range(CHUNKS):
+            for z in range(2):
+                fp8_by_fp4(y_bank[c], wy[z], wy_s[z], xt[z], xt_s, z, c, z == 0, False)
+            for j in range(PACK):
+                nc.tensor.matmul_mx(
+                    out=y_bank[c][:, j, :],
+                    lhsT=wb[:, cols2(j)].bitcast(E2M1),
+                    lhsT_scale=wb_s[:, cols(j)],
+                    rhs=hid_q[c][:].bitcast(E4M3),
+                    rhs_scale=hid_s[c][:],
+                    start=False,
+                    stop=j == PACK - 1,
+                )
+            y = tile("y%d" % c, [P, PACK, TC], F32)
+            nc.scalar.copy(out=y[:], in_=y_bank[c][:])
+            nc.sync.dma_start(out=out_rows[:, :, cols(c)], in_=y[:])
+            y_bf = tile("y_bf%d" % c, [P, TC, PACK], BF16)
+            nc.vector.tensor_copy(
+                out=y_bf[:].rearrange("p (b i) j -> p b j i", i=4),
+                in_=y[:].rearrange("p j (b i) -> p b j i", i=4),
+            )
+            y_q = tile("y_q%d" % c, [P, TC], U32)
+            nc.vector.quantize_mx(out=y_q[:].bitcast(E4M3), scales=y_s[:, cols(c)], in_=y_bf[:].rearrange("p t j -> p (t j)"))
+            nc.sync.dma_start(out=out_words[:, cols(c)], in_=y_q[:].bitcast(I32))
+        for q in range(4):
+            queue = nc.scalar if q % 2 == 0 else nc.sync
+            queue.dma_start(
+                out=out_2[0, 4 * q : 4 * q + 4, :].bitcast(I32),
+                in_=y_s[32 * q : 32 * q + 4, :].bitcast(I32),
+            )

@@ -45,21 +45,21 @@ def tile_mix_conditioned_hidden_pl_kernel(
                 in_=scales[:, 4 * q : 4 * q + 4, :].rearrange("z r c -> r z c").bitcast(I32),
             )
 
-        def load_e4m3(name, words, z):
+        def load_e4m3(queue, name, words, z):
             raw = tile(name, [P, W], U32)
-            nc.sync.dma_start(out=raw[:].bitcast(I32), in_=words[z].rearrange("p c r -> p (c r)").bitcast(I32))
+            queue.dma_start(out=raw[:].bitcast(I32), in_=words[z].rearrange("p c r -> p (c r)").bitcast(I32))
             return raw
 
-        def load_e2m1(name, words, z):
+        def load_e2m1(queue, name, words, z):
             raw = tile(name, [P, 2 * W], U8)
-            nc.sync.dma_start(out=raw[:].bitcast(I32), in_=words[z].bitcast(I32))
+            queue.dma_start(out=raw[:].bitcast(I32), in_=words[z].bitcast(I32))
             return raw
 
         def deal_e4m3(name, raw):
             dealt = tile(name, [P, W], U32)
             nc.vector.tensor_copy(
                 out=dealt[:].bitcast(I32).rearrange("p (j b i) -> p b j i", j=PACK, i=4),
-                in_=raw[:].bitcast(I32).rearrange("p (b i j) -> p b j i", j=PACK, i=4),
+                in_=raw.bitcast(I32).rearrange("p (b i j) -> p b j i", j=PACK, i=4),
             )
             return dealt
 
@@ -87,104 +87,138 @@ def tile_mix_conditioned_hidden_pl_kernel(
 
         wa_sraw = scale_tile("wa_sraw", 2)
         xt_s = scale_tile("xt_s", 2)
-        cq_s = scale_tile("cq_s", 1)
-        wc_sraw = scale_tile("wc_sraw", 1)
-        wy_sraw = scale_tile("wy_sraw", 2)
-        wb_sraw = scale_tile("wb_sraw", 1)
+        late_raw = scale_tile("late_raw", 2)
+        late_dealt = tile("late_dealt", [P, 3, W], U8)
+        nc.vector.memset(late_dealt[:, 2, :].bitcast(I32), 0)
+        late_s = scale_tile("late_s", 6)
 
-        wa_raw = [load_e4m3("wa_raw0", wa_words, 0)]
-        xt = [load_e2m1("xt0", xt_words, 0)]
+        xt = [load_e2m1(nc.sync, "xt0", xt_words, 0)]
+        wa_raw = [load_e4m3(nc.sync, "wa_raw0", wa_words, 0)]
         for q in range(4):
             load_scales(nc.scalar, wa_sraw, wa_scales, q)
-        for q in range(2):
+        for q in range(4):
             load_scales(nc.sync, xt_s, xt_scales, q)
-        for q in range(2, 4):
-            load_scales(nc.gpsimd, xt_s, xt_scales, q)
-        for q in range(2):
-            load_scales(nc.gpsimd, cq_s, cq_scales, q)
-        wa_raw.append(load_e4m3("wa_raw1", wa_words, 1))
-        xt.append(load_e2m1("xt1", xt_words, 1))
-        for q in range(4):
-            load_scales(nc.scalar, wc_sraw, wc_scales, q)
-        wc_raw = load_e4m3("wc_raw", wc_words, 0)
-        cq = load_e2m1("cq", cq_words, 0)
-        for q in range(2, 4):
-            load_scales(nc.sync, cq_s, cq_scales, q)
-        for q in range(4):
-            load_scales(nc.sync, wy_sraw, wy_scales, q)
-        wy_raw = [load_e4m3("wy_raw%d" % z, wy_words, z) for z in range(2)]
-        wb_raw = load_e2m1("wb_raw", wb_words, 0)
-        for q in range(4):
-            load_scales(nc.sync, wb_sraw, wb_scales, q)
+        nc.scalar.dma_start(out=late_raw[1:32:2, 0, :].bitcast(I32), in_=wc_scales[0].bitcast(I32))
+        nc.scalar.dma_start(out=late_raw[0:32:2, :, :].bitcast(I32), in_=wy_scales.rearrange("z q c -> q z c").bitcast(I32))
+        nc.scalar.dma_start(out=late_raw[1:32:2, 1, :].bitcast(I32), in_=wb_scales[0].bitcast(I32))
+        nc.scalar.dma_start(out=late_dealt[0:32:2, 2, :].bitcast(I32), in_=cq_scales[0].bitcast(I32))
+        wa_raw.append(load_e4m3(nc.sync, "wa_raw1", wa_words, 1))
+        xt.append(load_e2m1(nc.sync, "xt1", xt_words, 1))
+        wc_raw = load_e4m3(nc.scalar, "wc_raw", wc_words, 0)
+        cq = load_e2m1(nc.scalar, "cq", cq_words, 0)
+        wy_raw = tile("wy_raw", [P, 2, W], U32)
+        nc.scalar.dma_start(out=wy_raw[:].bitcast(I32), in_=wy_words.rearrange("z p c r -> p z (c r)").bitcast(I32))
+        wb_raw = load_e2m1(nc.scalar, "wb_raw", wb_words, 0)
 
         wa_s = [deal_scales("wa_s0", wa_sraw, 0)]
-        wa = [deal_e4m3("wa0", wa_raw[0])]
+        wa = [deal_e4m3("wa0", wa_raw[0][:])]
         wa_s.append(deal_scales("wa_s1", wa_sraw, 1))
-        wa.append(deal_e4m3("wa1", wa_raw[1]))
-        wc_s = deal_scales("wc_s", wc_sraw, 0)
-        wc = deal_e4m3("wc", wc_raw)
-        wy_s = [deal_scales("wy_s%d" % z, wy_sraw, z) for z in range(2)]
-        wy = [deal_e4m3("wy%d" % z, wy_raw[z]) for z in range(2)]
+        nc.vector.tensor_copy(
+            out=late_dealt[:, 0:2, :].rearrange("p z (j m) -> p z j m", j=PACK),
+            in_=late_raw[:].rearrange("p z (m j) -> p z j m", j=PACK),
+        )
+        for q in range(4):
+            nc.sync.dma_start(
+                out=late_s[32 * q : 32 * q + 4, :, :].rearrange("r s c -> r (s c)").bitcast(I32),
+                in_=late_dealt[8 * q : 8 * q + 8, :, :].rearrange("p s c -> p (s c)").bitcast(I32),
+            )
+        wa.append(deal_e4m3("wa1", wa_raw[1][:]))
+        wc = deal_e4m3("wc", wc_raw[:])
+        wy = [deal_e4m3("wy%d" % z, wy_raw[:, z, :]) for z in range(2)]
         wb = deal_e2m1("wb", wb_raw)
-        wb_s = deal_scales("wb_s", wb_sraw, 0)
+        wy_s = [late_s[:, 0, :], late_s[:, 1, :]]
+        cq_s = late_s[:, 2:3, :]
+        wc_s = late_s[:, 3, :]
+        wb_s = late_s[:, 4, :]
 
         z_bank = [psum.tile([P, PACK, TC], F32, name="z%d" % c) for c in range(CHUNKS)]
         y_bank = [psum.tile([P, PACK, TC], F32, name="y%d" % c) for c in range(CHUNKS)]
 
-        def fp8_by_fp4(bank, w, w_s, x, x_s, z, c, first, last):
-            for j in range(PACK):
-                nc.tensor.matmul_mx(
-                    out=bank[:, j, :],
-                    lhsT=w[:, cols(j)].bitcast(E4M3),
-                    lhsT_scale=w_s[:, cols(j)],
-                    rhs=x[:, cols2(c)].bitcast(E2M1),
-                    rhs_scale=x_s[:, z, cols(c)],
-                    start=first and j == 0,
-                    stop=last and j == PACK - 1,
-                )
+        def fp8_by_fp4(out, w, w_s, x, x_s, j, c, start, stop):
+            nc.tensor.matmul_mx(
+                out=out,
+                lhsT=w[:, cols(j)].bitcast(E4M3),
+                lhsT_scale=w_s[:, cols(j)],
+                rhs=x[:, cols2(c)].bitcast(E2M1),
+                rhs_scale=x_s[:, cols(c)],
+                start=start,
+                stop=stop,
+            )
 
         for z in range(2):
             for c in range(CHUNKS):
-                fp8_by_fp4(z_bank[c], wa[z], wa_s[z], xt[z], xt_s, z, c, z == 0, False)
-        hid_q = []
-        hid_s = []
+                for j in range(PACK):
+                    fp8_by_fp4(z_bank[c][:, j, :], wa[z], wa_s[z], xt[z], xt_s[:, z, :], j, c, z == 0 and j == 0, False)
         for c in range(CHUNKS):
-            fp8_by_fp4(z_bank[c], wc, wc_s, cq, cq_s, 0, c, False, True)
-            hid = tile("hid%d" % c, [P, TC, PACK], BF16)
-            nc.scalar.activation(out=hid[:], in_=z_bank[c][:].rearrange("p j t -> p t j"), func=ACT.Relu)
-            codes = tile("hid_q%d" % c, [P, TC], U32)
-            plane = tile("hid_s%d" % c, [P, TC], U8)
-            nc.vector.quantize_mx(out=codes[:].bitcast(E4M3), scales=plane[:], in_=hid[:].rearrange("p t j -> p (t j)"))
-            hid_q.append(codes)
-            hid_s.append(plane)
+            for j in range(PACK):
+                fp8_by_fp4(z_bank[c][:, j, :], wc, wc_s, cq, cq_s[:, 0, :], j, c, False, j == PACK - 1)
 
+        hid = [tile("hid%d" % c, [P, TC, PACK], BF16) for c in range(CHUNKS)]
+        hid_q = [tile("hid_q%d" % c, [P, TC], U32) for c in range(CHUNKS)]
+        hid_s = [tile("hid_s%d" % c, [P, TC], U8) for c in range(CHUNKS)]
+        y = [tile("y%d" % c, [P, PACK, TC], F32) for c in range(CHUNKS)]
+        y_q = tile("y_q", [P, T], U32)
+        y_s = tile("y_s", [P, T], U8)
         out_rows = out_0.rearrange("(p j) t -> p j t", j=PACK)
         out_words = out_1[0].rearrange("p c r -> p (c r)").bitcast(I32)
-        y_s = tile("y_s", [P, T], U8)
-        for c in range(CHUNKS):
-            for z in range(2):
-                fp8_by_fp4(y_bank[c], wy[z], wy_s[z], xt[z], xt_s, z, c, z == 0, False)
-            for j in range(PACK):
-                nc.tensor.matmul_mx(
-                    out=y_bank[c][:, j, :],
-                    lhsT=wb[:, cols2(j)].bitcast(E2M1),
-                    lhsT_scale=wb_s[:, cols(j)],
-                    rhs=hid_q[c][:].bitcast(E4M3),
-                    rhs_scale=hid_s[c][:],
-                    start=False,
-                    stop=j == PACK - 1,
-                )
-            y = tile("y%d" % c, [P, PACK, TC], F32)
-            nc.scalar.copy(out=y[:], in_=y_bank[c][:])
-            nc.sync.dma_start(out=out_rows[:, :, cols(c)], in_=y[:])
+
+        def relu_on_scalar(c):
+            nc.scalar.activation(out=hid[c][:], in_=z_bank[c][:].rearrange("p j t -> p t j"), func=ACT.Relu)
+
+        def relu_on_vector(c):
+            nc.vector.tensor_scalar_max(hid[c][:], z_bank[c][:].rearrange("p j t -> p t j"), 0.0)
+
+        def quantize_hid(c):
+            nc.vector.quantize_mx(
+                out=hid_q[c][:].bitcast(E4M3), scales=hid_s[c][:], in_=hid[c][:].rearrange("p t j -> p (t j)")
+            )
+
+        def second_layer(c):
+            for half, bank in enumerate((y_bank[c], z_bank[c])):
+                js = (2 * half, 2 * half + 1)
+                for z in range(2):
+                    for j in js:
+                        fp8_by_fp4(bank[:, j, :], wy[z], wy_s[z], xt[z], xt_s[:, z, :], j, c, z == 0 and j == js[0], False)
+                for j in js:
+                    nc.tensor.matmul_mx(
+                        out=bank[:, j, :],
+                        lhsT=wb[:, cols2(j)].bitcast(E2M1),
+                        lhsT_scale=wb_s[:, cols(j)],
+                        rhs=hid_q[c][:].bitcast(E4M3),
+                        rhs_scale=hid_s[c][:],
+                        start=False,
+                        stop=j == js[1],
+                    )
+                nc.scalar.copy(out=y[c][:, js[0] : js[1] + 1, :], in_=bank[:, js[0] : js[1] + 1, :])
+            nc.sync.dma_start(out=out_rows[:, :, cols(c)], in_=y[c][:])
             y_bf = tile("y_bf%d" % c, [P, TC, PACK], BF16)
             nc.vector.tensor_copy(
                 out=y_bf[:].rearrange("p (b i) j -> p b j i", i=4),
-                in_=y[:].rearrange("p j (b i) -> p b j i", i=4),
+                in_=y[c][:].rearrange("p j (b i) -> p b j i", i=4),
             )
-            y_q = tile("y_q%d" % c, [P, TC], U32)
-            nc.vector.quantize_mx(out=y_q[:].bitcast(E4M3), scales=y_s[:, cols(c)], in_=y_bf[:].rearrange("p t j -> p (t j)"))
-            nc.sync.dma_start(out=out_words[:, cols(c)], in_=y_q[:].bitcast(I32))
+            nc.vector.quantize_mx(
+                out=y_q[:, cols(c)].bitcast(E4M3), scales=y_s[:, cols(c)], in_=y_bf[:].rearrange("p t j -> p (t j)")
+            )
+
+        def store_words(first, last):
+            span = slice(first * TC, (last + 1) * TC)
+            nc.sync.dma_start(out=out_words[:, span], in_=y_q[:, span].bitcast(I32))
+
+        relu_on_scalar(0)
+        quantize_hid(0)
+        relu_on_scalar(1)
+        relu_on_vector(3)
+        quantize_hid(1)
+        relu_on_scalar(2)
+        quantize_hid(3)
+        quantize_hid(2)
+        second_layer(0)
+        second_layer(1)
+        store_words(0, 1)
+        second_layer(2)
+        store_words(2, 2)
+        second_layer(3)
+        store_words(3, 3)
         for q in range(4):
             queue = nc.scalar if q % 2 == 0 else nc.sync
             queue.dma_start(

@@ -12,13 +12,17 @@ U32 = mybir.dt.uint32
 U8 = mybir.dt.uint8
 E4M3 = mybir.dt.float8_e4m3fn_x4
 E2M1 = mybir.dt.float4_e2m1fn_x4
-ACT = mybir.ActivationFunctionType
+RELU = mybir.ActivationFunctionType.Relu
 
 P = 128
 PACK = 4
-W = 512
-TC = 128
-CHUNKS = T // TC
+WIDTH = 512
+CHUNK = 128
+CHUNKS = T // CHUNK
+LINE = 4
+ROWS = 16
+WARM_UP_PASSES = 2
+QUADRANTS = (0, 2, 1, 3)
 
 
 def tile_mix_conditioned_hidden_pl_kernel(
@@ -27,201 +31,247 @@ def tile_mix_conditioned_hidden_pl_kernel(
 ):
     nc = tc.nc
     with ExitStack() as ctx:
-        sb = ctx.enter_context(tc.tile_pool(name="sb", bufs=1))
+        sbuf = ctx.enter_context(tc.tile_pool(name="sbuf", bufs=1))
         psum = ctx.enter_context(tc.psum_pool(name="psum", bufs=1))
         ctx.enter_context(tc.manual_schedule())
 
         def tile(name, shape, dtype):
-            return sb.tile(shape, dtype, name=name, align_bytes=64)
+            return sbuf.tile(shape, dtype, name=name, align_bytes=64)
 
-        def scale_tile(name, passes):
-            plane = tile(name, [P, passes, W], U8)
-            nc.vector.memset(plane[:].rearrange("p z c -> p (z c)").bitcast(I32), 0)
-            return plane
+        def zeroed(name, passes):
+            scales = tile(name, [P, passes, WIDTH], U8)
+            nc.vector.memset(scales[:].rearrange("p z c -> p (z c)").bitcast(I32), 0)
+            return scales
 
-        def load_scales(queue, plane, scales, q):
-            queue.dma_start(
-                out=plane[32 * q : 32 * q + 4, :, :].bitcast(I32),
-                in_=scales[:, 4 * q : 4 * q + 4, :].rearrange("z r c -> r z c").bitcast(I32),
-            )
+        def live_rows(quadrant):
+            return slice(32 * quadrant, 32 * quadrant + 4)
 
-        def load_e4m3(queue, name, words, z):
-            raw = tile(name, [P, W], U32)
-            queue.dma_start(out=raw[:].bitcast(I32), in_=words[z].rearrange("p c r -> p (c r)").bitcast(I32))
+        def load_planes(queue, planes, scales):
+            for quadrant in QUADRANTS:
+                rows = scales[:, 4 * quadrant : 4 * quadrant + 4, :].rearrange("z i c -> i z c")
+                queue.dma_start(out=planes[live_rows(quadrant), :, :].bitcast(I32), in_=rows.bitcast(I32))
+
+        def load_e4m3(queue, name, words):
+            raw = tile(name, [P, words.shape[0], WIDTH], U32)
+            queue.dma_start(out=raw[:].bitcast(I32), in_=words.rearrange("z p c i -> p z (c i)").bitcast(I32))
             return raw
 
-        def load_e2m1(queue, name, words, z):
-            raw = tile(name, [P, 2 * W], U8)
-            queue.dma_start(out=raw[:].bitcast(I32), in_=words[z].bitcast(I32))
+        def load_e2m1(queue, name, words):
+            raw = tile(name, [P, 2 * WIDTH], U8)
+            queue.dma_start(out=raw[:].bitcast(I32), in_=words.bitcast(I32))
             return raw
 
         def deal_e4m3(name, raw):
-            dealt = tile(name, [P, W], U32)
+            dealt = tile(name, [P, WIDTH], U32)
             nc.vector.tensor_copy(
-                out=dealt[:].bitcast(I32).rearrange("p (j b i) -> p b j i", j=PACK, i=4),
-                in_=raw.bitcast(I32).rearrange("p (b i j) -> p b j i", j=PACK, i=4),
+                out=dealt[:].bitcast(I32).rearrange("p (j b i) -> p b j i", j=PACK, i=LINE),
+                in_=raw.bitcast(I32).rearrange("p (b i j) -> p b j i", j=PACK, i=LINE),
             )
             return dealt
 
         def deal_e2m1(name, raw):
-            dealt = tile(name, [P, 2 * W], U8)
+            dealt = tile(name, [P, 2 * WIDTH], U8)
             nc.vector.tensor_copy(
                 out=dealt[:].rearrange("p (j m e) -> p j m e", j=PACK, e=2),
                 in_=raw[:].rearrange("p (m j e) -> p j m e", j=PACK, e=2),
             )
             return dealt
 
-        def deal_scales(name, plane, z):
-            dealt = tile(name, [P, W], U8)
+        def deal_plane(name, raw):
+            dealt = tile(name, [P, WIDTH], U8)
             nc.vector.tensor_copy(
                 out=dealt[:].rearrange("p (j m) -> p j m", j=PACK),
-                in_=plane[:, z, :].rearrange("p (m j) -> p j m", j=PACK),
+                in_=raw.rearrange("p (m j) -> p j m", j=PACK),
             )
             return dealt
 
-        def cols(i):
-            return slice(i * P, (i + 1) * P)
+        def columns(index):
+            return slice(index * P, (index + 1) * P)
 
-        def cols2(i):
-            return slice(2 * i * P, 2 * (i + 1) * P)
+        def e2m1_bytes(index):
+            return slice(2 * index * P, 2 * (index + 1) * P)
 
-        wa_sraw = scale_tile("wa_sraw", 2)
-        xt_s = scale_tile("xt_s", 2)
-        late_raw = scale_tile("late_raw", 2)
-        late_dealt = tile("late_dealt", [P, 3, W], U8)
-        nc.vector.memset(late_dealt[:, 2, :].bitcast(I32), 0)
-        late_s = scale_tile("late_s", 6)
+        wa_planes_raw = zeroed("wa_planes_raw", 2)
+        xt_planes = zeroed("xt_planes", 2)
+        staged_raw = zeroed("staged_raw", 2)
+        staged = tile("staged", [P, 2 * WIDTH + WIDTH // 2], U8)
+        late_planes = zeroed("late_planes", 5)
 
-        xt = [load_e2m1(nc.sync, "xt0", xt_words, 0)]
-        wa_raw = [load_e4m3(nc.sync, "wa_raw0", wa_words, 0)]
-        for q in range(4):
-            load_scales(nc.scalar, wa_sraw, wa_scales, q)
-        for q in range(4):
-            load_scales(nc.sync, xt_s, xt_scales, q)
-        nc.scalar.dma_start(out=late_raw[1:32:2, 0, :].bitcast(I32), in_=wc_scales[0].bitcast(I32))
-        nc.scalar.dma_start(out=late_raw[0:32:2, :, :].bitcast(I32), in_=wy_scales.rearrange("z q c -> q z c").bitcast(I32))
-        nc.scalar.dma_start(out=late_raw[1:32:2, 1, :].bitcast(I32), in_=wb_scales[0].bitcast(I32))
-        nc.scalar.dma_start(out=late_dealt[0:32:2, 2, :].bitcast(I32), in_=cq_scales[0].bitcast(I32))
-        wa_raw.append(load_e4m3(nc.sync, "wa_raw1", wa_words, 1))
-        xt.append(load_e2m1(nc.sync, "xt1", xt_words, 1))
-        wc_raw = load_e4m3(nc.scalar, "wc_raw", wc_words, 0)
-        cq = load_e2m1(nc.scalar, "cq", cq_words, 0)
-        wy_raw = tile("wy_raw", [P, 2, W], U32)
-        nc.scalar.dma_start(out=wy_raw[:].bitcast(I32), in_=wy_words.rearrange("z p c r -> p z (c r)").bitcast(I32))
-        wb_raw = load_e2m1(nc.scalar, "wb_raw", wb_words, 0)
-
-        wa_s = [deal_scales("wa_s0", wa_sraw, 0)]
-        wa = [deal_e4m3("wa0", wa_raw[0][:])]
-        wa_s.append(deal_scales("wa_s1", wa_sraw, 1))
-        nc.vector.tensor_copy(
-            out=late_dealt[:, 0:2, :].rearrange("p z (j m) -> p z j m", j=PACK),
-            in_=late_raw[:].rearrange("p z (m j) -> p z j m", j=PACK),
+        xt = [load_e2m1(nc.sync, "xt0", xt_words[0])]
+        wa_raw = [load_e4m3(nc.sync, "wa_raw0", wa_words[0:1])]
+        load_planes(nc.scalar, wa_planes_raw, wa_scales)
+        load_planes(nc.sync, xt_planes, xt_scales)
+        even, odd = slice(0, 2 * ROWS, 2), slice(1, 2 * ROWS, 2)
+        nc.scalar.dma_start(out=staged_raw[odd, 0, :].bitcast(I32), in_=wc_scales[0].bitcast(I32))
+        nc.scalar.dma_start(
+            out=staged_raw[even, :, :].bitcast(I32), in_=wy_scales.rearrange("z q c -> q z c").bitcast(I32)
         )
-        for q in range(4):
+        nc.scalar.dma_start(out=staged_raw[odd, 1, :].bitcast(I32), in_=wb_scales[0].bitcast(I32))
+        nc.scalar.dma_start(
+            out=staged[: 2 * ROWS, 2 * WIDTH :].bitcast(I32),
+            in_=cq_scales[0].rearrange("q (g c) -> (q g) c", g=2).bitcast(I32),
+        )
+        wa_raw.append(load_e4m3(nc.sync, "wa_raw1", wa_words[1:2]))
+        xt.append(load_e2m1(nc.sync, "xt1", xt_words[1]))
+        wc_raw = load_e4m3(nc.scalar, "wc_raw", wc_words)
+        cq = load_e2m1(nc.scalar, "cq", cq_words[0])
+        wy_raw = load_e4m3(nc.scalar, "wy_raw", wy_words)
+
+        wa_planes = [deal_plane("wa_plane0", wa_planes_raw[:, 0, :])]
+        wa = [deal_e4m3("wa0", wa_raw[0][:, 0, :])]
+        wa_planes.append(deal_plane("wa_plane1", wa_planes_raw[:, 1, :]))
+        nc.vector.tensor_copy(
+            out=staged[:, : 2 * WIDTH].rearrange("p (z j m) -> p z j m", z=2, j=PACK),
+            in_=staged_raw[:].rearrange("p z (m j) -> p z j m", j=PACK),
+        )
+        for quadrant in QUADRANTS:
             nc.sync.dma_start(
-                out=late_s[32 * q : 32 * q + 4, :, :].rearrange("r s c -> r (s c)").bitcast(I32),
-                in_=late_dealt[8 * q : 8 * q + 8, :, :].rearrange("p s c -> p (s c)").bitcast(I32),
+                out=late_planes[live_rows(quadrant), :, :].rearrange("i s c -> i (s c)").bitcast(I32),
+                in_=staged[8 * quadrant : 8 * quadrant + 8, :].bitcast(I32),
             )
-        wa.append(deal_e4m3("wa1", wa_raw[1][:]))
-        wc = deal_e4m3("wc", wc_raw[:])
+        wb_raw = load_e2m1(nc.sync, "wb_raw", wb_words[0])
+        wa.append(deal_e4m3("wa1", wa_raw[1][:, 0, :]))
+        wc = deal_e4m3("wc", wc_raw[:, 0, :])
         wy = [deal_e4m3("wy%d" % z, wy_raw[:, z, :]) for z in range(2)]
         wb = deal_e2m1("wb", wb_raw)
-        wy_s = [late_s[:, 0, :], late_s[:, 1, :]]
-        cq_s = late_s[:, 2:3, :]
-        wc_s = late_s[:, 3, :]
-        wb_s = late_s[:, 4, :]
 
-        z_bank = [psum.tile([P, PACK, TC], F32, name="z%d" % c) for c in range(CHUNKS)]
-        y_bank = [psum.tile([P, PACK, TC], F32, name="y%d" % c) for c in range(CHUNKS)]
+        late = late_planes[:].rearrange("p s c -> p (s c)").rearrange("p (g c) -> p g c", g=2)
+        wy_planes = [late[:, 0, :WIDTH], late[:, 0, WIDTH : 2 * WIDTH]]
+        wc_plane = late[:, 1, :WIDTH]
+        wb_plane = late[:, 1, WIDTH : 2 * WIDTH]
+        cq_halves = [late[:, g, 2 * WIDTH :] for g in range(2)]
 
-        def fp8_by_fp4(out, w, w_s, x, x_s, j, c, start, stop):
+        z_bank = [psum.tile([P, PACK, CHUNK], F32, name="z_bank%d" % c) for c in range(CHUNKS)]
+        y_bank = [psum.tile([P, PACK, CHUNK], F32, name="y_bank%d" % c) for c in range(CHUNKS)]
+
+        def weights_by_tokens(bank, j, c, weights, weights_plane, tokens, tokens_scales, start, stop):
             nc.tensor.matmul_mx(
-                out=out,
-                lhsT=w[:, cols(j)].bitcast(E4M3),
-                lhsT_scale=w_s[:, cols(j)],
-                rhs=x[:, cols2(c)].bitcast(E2M1),
-                rhs_scale=x_s[:, cols(c)],
+                out=bank[:, j, :],
+                lhsT=weights[:, columns(j)].bitcast(E4M3),
+                lhsT_scale=weights_plane[:, columns(j)],
+                rhs=tokens[:, e2m1_bytes(c)].bitcast(E2M1),
+                rhs_scale=tokens_scales,
                 start=start,
                 stop=stop,
+            )
+
+        for repeat in range(WARM_UP_PASSES):
+            nc.tensor.matmul_mx(
+                out=y_bank[CHUNKS - 1][:].rearrange("p j t -> p (j t)"),
+                lhsT=wa_raw[0][:, 0, columns(0)].bitcast(E4M3),
+                lhsT_scale=wa_planes_raw[:, 0, columns(0)],
+                rhs=xt[0][:].bitcast(E2M1),
+                rhs_scale=wa_planes_raw[:, 0, :],
+                start=True,
+                stop=True,
             )
 
         for z in range(2):
             for c in range(CHUNKS):
                 for j in range(PACK):
-                    fp8_by_fp4(z_bank[c][:, j, :], wa[z], wa_s[z], xt[z], xt_s[:, z, :], j, c, z == 0 and j == 0, False)
+                    weights_by_tokens(
+                        z_bank[c], j, c, wa[z], wa_planes[z], xt[z], xt_planes[:, z, columns(c)],
+                        start=z == 0 and j == 0, stop=False,
+                    )
         for c in range(CHUNKS):
             for j in range(PACK):
-                fp8_by_fp4(z_bank[c][:, j, :], wc, wc_s, cq, cq_s[:, 0, :], j, c, False, j == PACK - 1)
+                weights_by_tokens(
+                    z_bank[c], j, c, wc, wc_plane, cq, cq_halves[c // 2][:, columns(c % 2)],
+                    start=False, stop=j == PACK - 1,
+                )
 
-        hid = [tile("hid%d" % c, [P, TC, PACK], BF16) for c in range(CHUNKS)]
-        hid_q = [tile("hid_q%d" % c, [P, TC], U32) for c in range(CHUNKS)]
-        hid_s = [tile("hid_s%d" % c, [P, TC], U8) for c in range(CHUNKS)]
-        y = [tile("y%d" % c, [P, PACK, TC], F32) for c in range(CHUNKS)]
-        y_q = tile("y_q", [P, T], U32)
-        y_s = tile("y_s", [P, T], U8)
-        out_rows = out_0.rearrange("(p j) t -> p j t", j=PACK)
-        out_words = out_1[0].rearrange("p c r -> p (c r)").bitcast(I32)
+        hid = [tile("hid%d" % c, [P, CHUNK, PACK], BF16) for c in range(CHUNKS)]
+        hid_codes = [tile("hid_codes%d" % c, [P, CHUNK], U32) for c in range(CHUNKS)]
+        hid_plane = [tile("hid_plane%d" % c, [P, CHUNK], U8) for c in range(CHUNKS)]
 
-        def relu_on_scalar(c):
-            nc.scalar.activation(out=hid[c][:], in_=z_bank[c][:].rearrange("p j t -> p t j"), func=ACT.Relu)
-
-        def relu_on_vector(c):
-            nc.vector.tensor_scalar_max(hid[c][:], z_bank[c][:].rearrange("p j t -> p t j"), 0.0)
+        def z_by_token(c):
+            return z_bank[c][:].rearrange("p j t -> p t j")
 
         def quantize_hid(c):
             nc.vector.quantize_mx(
-                out=hid_q[c][:].bitcast(E4M3), scales=hid_s[c][:], in_=hid[c][:].rearrange("p t j -> p (t j)")
+                out=hid_codes[c][:].bitcast(E4M3),
+                scales=hid_plane[c][:],
+                in_=hid[c][:].rearrange("p t j -> p (t j)"),
             )
 
-        def second_layer(c):
-            for half, bank in enumerate((y_bank[c], z_bank[c])):
-                js = (2 * half, 2 * half + 1)
-                for z in range(2):
-                    for j in js:
-                        fp8_by_fp4(bank[:, j, :], wy[z], wy_s[z], xt[z], xt_s[:, z, :], j, c, z == 0 and j == js[0], False)
-                for j in js:
-                    nc.tensor.matmul_mx(
-                        out=bank[:, j, :],
-                        lhsT=wb[:, cols2(j)].bitcast(E2M1),
-                        lhsT_scale=wb_s[:, cols(j)],
-                        rhs=hid_q[c][:].bitcast(E4M3),
-                        rhs_scale=hid_s[c][:],
-                        start=False,
-                        stop=j == js[1],
-                    )
-                nc.scalar.copy(out=y[c][:, js[0] : js[1] + 1, :], in_=bank[:, js[0] : js[1] + 1, :])
-            nc.sync.dma_start(out=out_rows[:, :, cols(c)], in_=y[c][:])
-            y_bf = tile("y_bf%d" % c, [P, TC, PACK], BF16)
-            nc.vector.tensor_copy(
-                out=y_bf[:].rearrange("p (b i) j -> p b j i", i=4),
-                in_=y[c][:].rearrange("p j (b i) -> p b j i", i=4),
-            )
-            nc.vector.quantize_mx(
-                out=y_q[:, cols(c)].bitcast(E4M3), scales=y_s[:, cols(c)], in_=y_bf[:].rearrange("p t j -> p (t j)")
-            )
-
-        def store_words(first, last):
-            span = slice(first * TC, (last + 1) * TC)
-            nc.sync.dma_start(out=out_words[:, span], in_=y_q[:, span].bitcast(I32))
-
-        relu_on_scalar(0)
+        last = CHUNKS - 1
+        nc.scalar.activation(out=hid[0][:], in_=z_by_token(0), func=RELU)
         quantize_hid(0)
-        relu_on_scalar(1)
-        relu_on_vector(3)
+        nc.scalar.activation(out=hid[1][:], in_=z_by_token(1), func=RELU)
+        nc.vector.tensor_scalar_max(hid[last][:], z_by_token(last), 0.0)
         quantize_hid(1)
-        relu_on_scalar(2)
-        quantize_hid(3)
+        nc.scalar.activation(out=hid[2][:], in_=z_by_token(2), func=RELU)
+        quantize_hid(last)
         quantize_hid(2)
-        second_layer(0)
-        second_layer(1)
-        store_words(0, 1)
-        second_layer(2)
-        store_words(2, 2)
-        second_layer(3)
-        store_words(3, 3)
-        for q in range(4):
-            queue = nc.scalar if q % 2 == 0 else nc.sync
+
+        y_codes = tile("y_codes", [P, T], U32)
+        y_plane = tile("y_plane", [P, T], U8)
+        out_rows = out_0.rearrange("(p j) t -> p j t", j=PACK)
+        out_words = out_1[0].rearrange("p c i -> p (c i)").bitcast(I32)
+
+        y = [tile("y%d" % c, [P, PACK, CHUNK], F32) for c in range(CHUNKS)]
+
+        def pair_bank(c, first):
+            return y_bank[c] if first == 0 else z_bank[c]
+
+        def skip_product(c, first):
+            for z in range(2):
+                for j in (first, first + 1):
+                    weights_by_tokens(
+                        pair_bank(c, first), j, c, wy[z], wy_planes[z], xt[z], xt_planes[:, z, columns(c)],
+                        start=z == 0 and j == first, stop=False,
+                    )
+
+        def hidden_product(c, first):
+            bank = pair_bank(c, first)
+            for j in (first, first + 1):
+                nc.tensor.matmul_mx(
+                    out=bank[:, j, :],
+                    lhsT=wb[:, e2m1_bytes(j)].bitcast(E2M1),
+                    lhsT_scale=wb_plane[:, columns(j)],
+                    rhs=hid_codes[c][:].bitcast(E4M3),
+                    rhs_scale=hid_plane[c][:],
+                    start=False,
+                    stop=j == first + 1,
+                )
+            nc.scalar.copy(out=y[c][:, first : first + 2, :], in_=bank[:, first : first + 2, :])
+
+        def hand_out(c):
+            nc.sync.dma_start(out=out_rows[:, :, columns(c)], in_=y[c][:])
+
+            half = CHUNK // 2
+            y_grouped = [tile("y_grouped%d_%d" % (c, h), [P, half, PACK], BF16) for h in range(2)]
+            for h in range(2):
+                nc.vector.tensor_copy(
+                    out=y_grouped[h][:].rearrange("p (b i) j -> p b j i", i=LINE),
+                    in_=y[c][:, :, h * half : (h + 1) * half].rearrange("p j (b i) -> p b j i", i=LINE),
+                )
+            for h in range(2):
+                tokens = slice(c * CHUNK + h * half, c * CHUNK + (h + 1) * half)
+                nc.vector.quantize_mx(
+                    out=y_codes[:, tokens].bitcast(E4M3),
+                    scales=y_plane[:, tokens],
+                    in_=y_grouped[h][:].rearrange("p t j -> p (t j)"),
+                )
+
+        def store_words(first_chunk, last_chunk):
+            tokens = slice(first_chunk * CHUNK, (last_chunk + 1) * CHUNK)
+            nc.sync.dma_start(out=out_words[:, tokens], in_=y_codes[:, tokens].bitcast(I32))
+
+        skip_product(0, 0)
+        skip_product(0, 2)
+        hidden_product(0, 0)
+        hidden_product(0, 2)
+        hand_out(0)
+        for c in range(1, CHUNKS):
+            for first in (0, 2):
+                skip_product(c, first)
+                hidden_product(c, first)
+            hand_out(c)
+            store_words(0 if c == 1 else c, c)
+        for quadrant in range(4):
+            queue = nc.scalar if quadrant % 2 == 0 else nc.sync
             queue.dma_start(
-                out=out_2[0, 4 * q : 4 * q + 4, :].bitcast(I32),
-                in_=y_s[32 * q : 32 * q + 4, :].bitcast(I32),
+                out=out_2[0, 4 * quadrant : 4 * quadrant + 4, :].bitcast(I32),
+                in_=y_plane[live_rows(quadrant), :].bitcast(I32),
             )

from contextlib import ExitStack

import concourse.mybir as mybir

K, L, T, R, N = 1024, 512, 512, 512, 512
FLOPS = 2 * T * (R * (K + L) + N * (R + K))

F32 = mybir.dt.float32
BF16 = mybir.dt.bfloat16
I32 = mybir.dt.int32
U32 = mybir.dt.uint32
U8 = mybir.dt.uint8
E4M3 = mybir.dt.float8_e4m3fn_x4
E2M1 = mybir.dt.float4_e2m1fn_x4
RELU = mybir.ActivationFunctionType.Relu

P = 128
PACK = 4
WIDTH = 512
CHUNK = 128
CHUNKS = T // CHUNK
LINE = 4
ROWS = 16
WARM_UP_PASSES = 2
QUADRANTS = (0, 2, 1, 3)


def tile_mix_conditioned_hidden_pl_kernel(
    tc, xt_words, xt_scales, wa_words, wa_scales, cq_words, cq_scales, wc_words, wc_scales,
    wb_words, wb_scales, wy_words, wy_scales, out_0, out_1, out_2,
):
    nc = tc.nc
    with ExitStack() as ctx:
        sbuf = ctx.enter_context(tc.tile_pool(name="sbuf", bufs=1))
        psum = ctx.enter_context(tc.psum_pool(name="psum", bufs=1))
        ctx.enter_context(tc.manual_schedule())

        def tile(name, shape, dtype):
            return sbuf.tile(shape, dtype, name=name, align_bytes=64)

        def zeroed(name, passes):
            scales = tile(name, [P, passes, WIDTH], U8)
            nc.vector.memset(scales[:].rearrange("p z c -> p (z c)").bitcast(I32), 0)
            return scales

        def live_rows(quadrant):
            return slice(32 * quadrant, 32 * quadrant + 4)

        def load_planes(queue, planes, scales):
            for quadrant in QUADRANTS:
                rows = scales[:, 4 * quadrant : 4 * quadrant + 4, :].rearrange("z i c -> i z c")
                queue.dma_start(out=planes[live_rows(quadrant), :, :].bitcast(I32), in_=rows.bitcast(I32))

        def load_e4m3(queue, name, words):
            raw = tile(name, [P, words.shape[0], WIDTH], U32)
            queue.dma_start(out=raw[:].bitcast(I32), in_=words.rearrange("z p c i -> p z (c i)").bitcast(I32))
            return raw

        def load_e2m1(queue, name, words):
            raw = tile(name, [P, 2 * WIDTH], U8)
            queue.dma_start(out=raw[:].bitcast(I32), in_=words.bitcast(I32))
            return raw

        def deal_e4m3(name, raw):
            dealt = tile(name, [P, WIDTH], U32)
            nc.vector.tensor_copy(
                out=dealt[:].bitcast(I32).rearrange("p (j b i) -> p b j i", j=PACK, i=LINE),
                in_=raw.bitcast(I32).rearrange("p (b i j) -> p b j i", j=PACK, i=LINE),
            )
            return dealt

        def deal_e2m1(name, raw):
            dealt = tile(name, [P, 2 * WIDTH], U8)
            nc.vector.tensor_copy(
                out=dealt[:].rearrange("p (j m e) -> p j m e", j=PACK, e=2),
                in_=raw[:].rearrange("p (m j e) -> p j m e", j=PACK, e=2),
            )
            return dealt

        def deal_plane(name, raw):
            dealt = tile(name, [P, WIDTH], U8)
            nc.vector.tensor_copy(
                out=dealt[:].rearrange("p (j m) -> p j m", j=PACK),
                in_=raw.rearrange("p (m j) -> p j m", j=PACK),
            )
            return dealt

        def columns(index):
            return slice(index * P, (index + 1) * P)

        def e2m1_bytes(index):
            return slice(2 * index * P, 2 * (index + 1) * P)

        wa_planes_raw = zeroed("wa_planes_raw", 2)
        xt_planes = zeroed("xt_planes", 2)
        staged_raw = zeroed("staged_raw", 2)
        staged = tile("staged", [P, 2 * WIDTH + WIDTH // 2], U8)
        late_planes = zeroed("late_planes", 5)

        xt = [load_e2m1(nc.sync, "xt0", xt_words[0])]
        wa_raw = [load_e4m3(nc.sync, "wa_raw0", wa_words[0:1])]
        load_planes(nc.scalar, wa_planes_raw, wa_scales)
        load_planes(nc.sync, xt_planes, xt_scales)
        even, odd = slice(0, 2 * ROWS, 2), slice(1, 2 * ROWS, 2)
        nc.scalar.dma_start(out=staged_raw[odd, 0, :].bitcast(I32), in_=wc_scales[0].bitcast(I32))
        nc.scalar.dma_start(
            out=staged_raw[even, :, :].bitcast(I32), in_=wy_scales.rearrange("z q c -> q z c").bitcast(I32)
        )
        nc.scalar.dma_start(out=staged_raw[odd, 1, :].bitcast(I32), in_=wb_scales[0].bitcast(I32))
        nc.scalar.dma_start(
            out=staged[: 2 * ROWS, 2 * WIDTH :].bitcast(I32),
            in_=cq_scales[0].rearrange("q (g c) -> (q g) c", g=2).bitcast(I32),
        )
        wa_raw.append(load_e4m3(nc.sync, "wa_raw1", wa_words[1:2]))
        xt.append(load_e2m1(nc.sync, "xt1", xt_words[1]))
        wc_raw = load_e4m3(nc.scalar, "wc_raw", wc_words)
        cq = load_e2m1(nc.scalar, "cq", cq_words[0])
        wy_raw = load_e4m3(nc.scalar, "wy_raw", wy_words)

        wa_planes = [deal_plane("wa_plane0", wa_planes_raw[:, 0, :])]
        wa = [deal_e4m3("wa0", wa_raw[0][:, 0, :])]
        wa_planes.append(deal_plane("wa_plane1", wa_planes_raw[:, 1, :]))
        nc.vector.tensor_copy(
            out=staged[:, : 2 * WIDTH].rearrange("p (z j m) -> p z j m", z=2, j=PACK),
            in_=staged_raw[:].rearrange("p z (m j) -> p z j m", j=PACK),
        )
        for quadrant in QUADRANTS:
            nc.sync.dma_start(
                out=late_planes[live_rows(quadrant), :, :].rearrange("i s c -> i (s c)").bitcast(I32),
                in_=staged[8 * quadrant : 8 * quadrant + 8, :].bitcast(I32),
            )
        wb_raw = load_e2m1(nc.sync, "wb_raw", wb_words[0])
        wa.append(deal_e4m3("wa1", wa_raw[1][:, 0, :]))
        wc = deal_e4m3("wc", wc_raw[:, 0, :])
        wy = [deal_e4m3("wy%d" % z, wy_raw[:, z, :]) for z in range(2)]
        wb = deal_e2m1("wb", wb_raw)

        late = late_planes[:].rearrange("p s c -> p (s c)").rearrange("p (g c) -> p g c", g=2)
        wy_planes = [late[:, 0, :WIDTH], late[:, 0, WIDTH : 2 * WIDTH]]
        wc_plane = late[:, 1, :WIDTH]
        wb_plane = late[:, 1, WIDTH : 2 * WIDTH]
        cq_halves = [late[:, g, 2 * WIDTH :] for g in range(2)]

        z_bank = [psum.tile([P, PACK, CHUNK], F32, name="z_bank%d" % c) for c in range(CHUNKS)]
        y_bank = [psum.tile([P, PACK, CHUNK], F32, name="y_bank%d" % c) for c in range(CHUNKS)]

        def weights_by_tokens(bank, j, c, weights, weights_plane, tokens, tokens_scales, start, stop):
            nc.tensor.matmul_mx(
                out=bank[:, j, :],
                lhsT=weights[:, columns(j)].bitcast(E4M3),
                lhsT_scale=weights_plane[:, columns(j)],
                rhs=tokens[:, e2m1_bytes(c)].bitcast(E2M1),
                rhs_scale=tokens_scales,
                start=start,
                stop=stop,
            )

        for repeat in range(WARM_UP_PASSES):
            nc.tensor.matmul_mx(
                out=y_bank[CHUNKS - 1][:].rearrange("p j t -> p (j t)"),
                lhsT=wa_raw[0][:, 0, columns(0)].bitcast(E4M3),
                lhsT_scale=wa_planes_raw[:, 0, columns(0)],
                rhs=xt[0][:].bitcast(E2M1),
                rhs_scale=wa_planes_raw[:, 0, :],
                start=True,
                stop=True,
            )

        for z in range(2):
            for c in range(CHUNKS):
                for j in range(PACK):
                    weights_by_tokens(
                        z_bank[c], j, c, wa[z], wa_planes[z], xt[z], xt_planes[:, z, columns(c)],
                        start=z == 0 and j == 0, stop=False,
                    )
        for c in range(CHUNKS):
            for j in range(PACK):
                weights_by_tokens(
                    z_bank[c], j, c, wc, wc_plane, cq, cq_halves[c // 2][:, columns(c % 2)],
                    start=False, stop=j == PACK - 1,
                )

        hid = [tile("hid%d" % c, [P, CHUNK, PACK], BF16) for c in range(CHUNKS)]
        hid_codes = [tile("hid_codes%d" % c, [P, CHUNK], U32) for c in range(CHUNKS)]
        hid_plane = [tile("hid_plane%d" % c, [P, CHUNK], U8) for c in range(CHUNKS)]

        def z_by_token(c):
            return z_bank[c][:].rearrange("p j t -> p t j")

        def quantize_hid(c):
            nc.vector.quantize_mx(
                out=hid_codes[c][:].bitcast(E4M3),
                scales=hid_plane[c][:],
                in_=hid[c][:].rearrange("p t j -> p (t j)"),
            )

        last = CHUNKS - 1
        nc.scalar.activation(out=hid[0][:], in_=z_by_token(0), func=RELU)
        quantize_hid(0)
        nc.scalar.activation(out=hid[1][:], in_=z_by_token(1), func=RELU)
        nc.vector.tensor_scalar_max(hid[last][:], z_by_token(last), 0.0)
        quantize_hid(1)
        nc.scalar.activation(out=hid[2][:], in_=z_by_token(2), func=RELU)
        quantize_hid(last)
        quantize_hid(2)

        y_codes = tile("y_codes", [P, T], U32)
        y_plane = tile("y_plane", [P, T], U8)
        out_rows = out_0.rearrange("(p j) t -> p j t", j=PACK)
        out_words = out_1[0].rearrange("p c i -> p (c i)").bitcast(I32)

        y = [tile("y%d" % c, [P, PACK, CHUNK], F32) for c in range(CHUNKS)]

        def pair_bank(c, first):
            return y_bank[c] if first == 0 else z_bank[c]

        def skip_product(c, first):
            for z in range(2):
                for j in (first, first + 1):
                    weights_by_tokens(
                        pair_bank(c, first), j, c, wy[z], wy_planes[z], xt[z], xt_planes[:, z, columns(c)],
                        start=z == 0 and j == first, stop=False,
                    )

        def hidden_product(c, first):
            bank = pair_bank(c, first)
            for j in (first, first + 1):
                nc.tensor.matmul_mx(
                    out=bank[:, j, :],
                    lhsT=wb[:, e2m1_bytes(j)].bitcast(E2M1),
                    lhsT_scale=wb_plane[:, columns(j)],
                    rhs=hid_codes[c][:].bitcast(E4M3),
                    rhs_scale=hid_plane[c][:],
                    start=False,
                    stop=j == first + 1,
                )
            nc.scalar.copy(out=y[c][:, first : first + 2, :], in_=bank[:, first : first + 2, :])

        def hand_out(c):
            nc.sync.dma_start(out=out_rows[:, :, columns(c)], in_=y[c][:])

            half = CHUNK // 2
            y_grouped = [tile("y_grouped%d_%d" % (c, h), [P, half, PACK], BF16) for h in range(2)]
            for h in range(2):
                nc.vector.tensor_copy(
                    out=y_grouped[h][:].rearrange("p (b i) j -> p b j i", i=LINE),
                    in_=y[c][:, :, h * half : (h + 1) * half].rearrange("p j (b i) -> p b j i", i=LINE),
                )
            for h in range(2):
                tokens = slice(c * CHUNK + h * half, c * CHUNK + (h + 1) * half)
                nc.vector.quantize_mx(
                    out=y_codes[:, tokens].bitcast(E4M3),
                    scales=y_plane[:, tokens],
                    in_=y_grouped[h][:].rearrange("p t j -> p (t j)"),
                )

        def store_words(first_chunk, last_chunk):
            tokens = slice(first_chunk * CHUNK, (last_chunk + 1) * CHUNK)
            nc.sync.dma_start(out=out_words[:, tokens], in_=y_codes[:, tokens].bitcast(I32))

        skip_product(0, 0)
        skip_product(0, 2)
        hidden_product(0, 0)
        hidden_product(0, 2)
        hand_out(0)
        for c in range(1, CHUNKS):
            for first in (0, 2):
                skip_product(c, first)
                hidden_product(c, first)
            hand_out(c)
            store_words(0 if c == 1 else c, c)
        for quadrant in range(4):
            queue = nc.scalar if quadrant % 2 == 0 else nc.sync
            queue.dma_start(
                out=out_2[0, 4 * quadrant : 4 * quadrant + 4, :].bitcast(I32),
                in_=y_plane[live_rows(quadrant), :].bitcast(I32),
            )
